import numpy as np
CORES = [6,14,22,30,38,46,54,62,70,78,86,94,102,110,118,126,196,197,198,199]
N = 20
G1 = [0,1,2,3,4,5,6,7,8,9,10,11,12,13,14,15,16,17,18,19]
ROOT1 = 1
G2 = [16,17,18,19]
def setup_inputs(rng):
    return {"x1": rng.standard_normal((N, 128, 512), dtype=np.float32), "x2": rng.standard_normal((N, 128, 4), dtype=np.float32)}
def reference(x1, x2):
    out = {}
    y = np.full((N, 128, 512), np.nan, x1.dtype)
    for r in G1:
        y[r] = x1[G1[ROOT1]]
    out["y1"] = y
    y = np.full((N, 128, 4), np.nan, x2.dtype)
    s = x2[G2].sum(axis=0, dtype=np.float64).astype(x2.dtype)
    for r in G2:
        y[r] = s
    out["y2"] = y
    return out

@@ -1,0 +1,119 @@
+from concourse.bass import DstId, RemoteDMATransfer
+
+NP = 16
+HALF = NP // 2
+
+SCRATCH = {
+    "buf": ("dram", [NP, 128, 32], "float32"),
+    "r": ("dram", [4, 128, 4], "float32"),
+    "rs": ("dram", [128, 4], "float32"),
+}
+SEMAPHORES = ["ldA", "ldB", "mine", "arrA", "arrB", "fwA", "fwB", "sent", "stA", "stB", "ld2", "got2", "res2", "st2"]
+
+
+def holder(p):
+    return 8 * p + (6 if p % 2 == 0 else 2)
+
+
+def rank_program(g, core, T, topo):
+    S = T.sem
+    cores = list(T.cores)
+    root = cores[T.tables["G1"][T.tables["ROOT1"]]]
+    far = [cores[r] for r in T.tables["G2"]]
+    near = [c for c in cores if c not in far and c != root]
+    arr = (S.arrA, S.arrB)
+    fw = (S.fwA, S.fwB)
+    st = (S.stA, S.stB)
+    queues = (g.sync, g.scalar)
+
+    def did(dst):
+        rid, pid = topo.addr(dst, core)
+        return DstId(rid=rid, pnc=pid)
+
+    def store(h, waits):
+        q = queues[h]
+        for sem, n in waits:
+            q.wait_ge(sem, n)
+        q.dma_start(T.y1[64 * h:64 * h + 64, :], T.buf[HALF * h:HALF * h + HALF]).then_inc(st[h], 16)
+
+    if core == root:
+        g.sync.dma_start(T.buf[0:HALF], T.x1[0:64, :]).then_inc(S.ldA, 16)
+        g.scalar.dma_start(T.buf[HALF:NP], T.x1[64:128, :]).then_inc(S.ldB, 16)
+        for h, ld in enumerate((S.ldA, S.ldB)):
+            g.wait_ge(ld, 16)
+            g.remote_dma_fused(
+                [RemoteDMATransfer(dst_ids=[did(holder(p))], dma_engine_mask=1 << (p % 8), remote_sem=S.mine,
+                                   srcs=[T.buf[p]], dsts=[T.buf[p]])
+                 for p in range(HALF * h, HALF * h + HALF)],
+                local_sem=S.sent)
+        g.sync.wait_ge(S.sent, NP)
+        g.sync.dma_start(T.y1[:], T.x1[:]).then_inc(S.stA, 16)
+        g.wait_ge(S.sent, NP)
+        g.wait_ge(S.stA, 16)
+        return
+
+    own = None
+    for p in range(NP):
+        if holder(p) == core:
+            own = p
+    if own is not None:
+        others = [c for c in near if c != core]
+        k = own % len(others)
+        dests = [far[own // 4]] + others[k:] + others[:k]
+        groups = [dests[e::8] for e in range(8)]
+        g.wait_ge(S.mine, 1)
+        g.remote_dma_fused(
+            [RemoteDMATransfer(dst_ids=[did(d) for d in grp], dma_engine_mask=1 << e, remote_sem=arr[own // HALF],
+                               srcs=[T.buf[own]], dsts=[T.buf[own] for d in grp])
+             for e, grp in enumerate(groups)],
+            local_sem=S.sent)
+        if core not in near:
+            g.wait_ge(S.sent, 8)
+            return
+
+    if core in near:
+        for h in range(2):
+            if own is not None and own // HALF == h:
+                store(h, [(S.mine, 1), (arr[h], HALF - 1)])
+            else:
+                store(h, [(arr[h], HALF)])
+        if own is not None:
+            g.wait_ge(S.sent, 8)
+        g.wait_ge(S.stA, 16)
+        g.wait_ge(S.stB, 16)
+        return
+
+    if core in far:
+        m = far.index(core)
+        sibs = [c for c in far if c != core]
+        g.sync.dma_start(T.r[m], T.x2[:]).then_inc(S.ld2, 16)
+        g.wait_ge(S.ld2, 16)
+        g.remote_dma_fused(
+            [RemoteDMATransfer(dst_ids=[did(s)], dma_engine_mask=1 << j, remote_sem=S.got2,
+                               srcs=[T.r[m]], dsts=[T.r[m]])
+             for j, s in enumerate(sibs)],
+            local_sem=S.sent)
+        g.wait_ge(S.got2, 3)
+        g.remote_dma_fused(
+            [RemoteDMATransfer(dst_ids=[did(far[(m + 1) % 4])], dma_engine_mask=1, remote_sem=S.res2,
+                               srcs=[T.r[j] for j in range(4)], dsts=[T.rs[:]], alu_op=1)],
+            local_sem=S.sent)
+        g.scalar.wait_ge(S.res2, 1)
+        g.scalar.dma_start(T.y2[:], T.rs[:]).then_inc(S.st2, 16)
+        hx = m // 2
+        g.wait_ge(arr[hx], 4)
+        g.remote_dma_fused(
+            [RemoteDMATransfer(dst_ids=[did(s) for s in sibs], dma_engine_mask=0xF << (4 * j), remote_sem=fw[hx],
+                               srcs=[T.buf[4 * m + j]], dsts=[T.buf[4 * m + j] for s in sibs])
+             for j in range(4)],
+            local_sem=S.sent)
+        for h in range(2):
+            if h == hx:
+                store(h, [(arr[h], 4), (fw[h], 16)])
+            else:
+                store(h, [(fw[h], 32)])
+        g.wait_ge(S.sent, 3 + 1 + 16)
+        g.wait_ge(S.st2, 16)
+        g.wait_ge(S.stA, 16)
+        g.wait_ge(S.stB, 16)
+        return

@@ -12,6 +12,8 @@ SEMAPHORES = ["ldA", "ldB", "mine", "arrA", "arrB", "fwA", "fwB", "sent", "stA",
 
 
 def holder(p):
+    if p == 0:
+        return 128 + 6
     return 8 * p + (6 if p % 2 == 0 else 2)
 
 
@@ -41,11 +43,12 @@ def rank_program(g, core, T, topo):
         g.scalar.dma_start(T.buf[HALF:NP], T.x1[64:128, :]).then_inc(S.ldB, 16)
         for h, ld in enumerate((S.ldA, S.ldB)):
             g.wait_ge(ld, 16)
-            g.remote_dma_fused(
-                [RemoteDMATransfer(dst_ids=[did(holder(p))], dma_engine_mask=1 << (p % 8), remote_sem=S.mine,
-                                   srcs=[T.buf[p]], dsts=[T.buf[p]])
-                 for p in range(HALF * h, HALF * h + HALF)],
-                local_sem=S.sent)
+            trs = []
+            for p in range(HALF * h, HALF * h + HALF):
+                to = [holder(p)] + ([far[p // 4]] if h == 1 else [])
+                trs.append(RemoteDMATransfer(dst_ids=[did(d) for d in to], dma_engine_mask=1 << (p % 8), remote_sem=S.mine,
+                                             srcs=[T.buf[p]], dsts=[T.buf[p] for d in to]))
+            g.remote_dma_fused(trs, local_sem=S.sent)
         g.sync.wait_ge(S.sent, NP)
         g.sync.dma_start(T.y1[:], T.x1[:]).then_inc(S.stA, 16)
         g.wait_ge(S.sent, NP)
@@ -59,7 +62,9 @@ def rank_program(g, core, T, topo):
     if own is not None:
         others = [c for c in near if c != core]
         k = own % len(others)
-        dests = [far[own // 4]] + others[k:] + others[:k]
+        dests = others[k:] + others[:k]
+        if own < HALF:
+            dests = [far[own // 4]] + dests
         groups = [dests[e::8] for e in range(8)]
         g.wait_ge(S.mine, 1)
         g.remote_dma_fused(
@@ -101,7 +106,8 @@ def rank_program(g, core, T, topo):
         g.scalar.wait_ge(S.res2, 1)
         g.scalar.dma_start(T.y2[:], T.rs[:]).then_inc(S.st2, 16)
         hx = m // 2
-        g.wait_ge(arr[hx], 4)
+        got = S.arrA if hx == 0 else S.mine
+        g.wait_ge(got, 4)
         g.remote_dma_fused(
             [RemoteDMATransfer(dst_ids=[did(s) for s in sibs], dma_engine_mask=0xF << (4 * j), remote_sem=fw[hx],
                                srcs=[T.buf[4 * m + j]], dsts=[T.buf[4 * m + j] for s in sibs])
@@ -109,7 +115,7 @@ def rank_program(g, core, T, topo):
             local_sem=S.sent)
         for h in range(2):
             if h == hx:
-                store(h, [(arr[h], 4), (fw[h], 16)])
+                store(h, [(got, 4), (fw[h], 16)])
             else:
                 store(h, [(fw[h], 32)])
         g.wait_ge(S.sent, 3 + 1 + 16)

@@ -2,6 +2,7 @@ from concourse.bass import DstId, RemoteDMATransfer
 
 NP = 16
 HALF = NP // 2
+ENG = (4, 4)
 
 SCRATCH = {
     "buf": ("dram", [NP, 128, 32], "float32"),
@@ -65,12 +66,13 @@ def rank_program(g, core, T, topo):
         dests = others[k:] + others[:k]
         if own < HALF:
             dests = [far[own // 4]] + dests
-        groups = [dests[e::8] for e in range(8)]
+        ne = ENG[own // HALF]
+        nt = 8 // ne
         g.wait_ge(S.mine, 1)
         g.remote_dma_fused(
-            [RemoteDMATransfer(dst_ids=[did(d) for d in grp], dma_engine_mask=1 << e, remote_sem=arr[own // HALF],
-                               srcs=[T.buf[own]], dsts=[T.buf[own] for d in grp])
-             for e, grp in enumerate(groups)],
+            [RemoteDMATransfer(dst_ids=[did(d) for d in dests[t::nt]], dma_engine_mask=((1 << ne) - 1) << (ne * t),
+                               remote_sem=arr[own // HALF], srcs=[T.buf[own]], dsts=[T.buf[own] for d in dests[t::nt]])
+             for t in range(nt)],
             local_sem=S.sent)
         if core not in near:
             g.wait_ge(S.sent, 8)
@@ -79,9 +81,9 @@ def rank_program(g, core, T, topo):
     if core in near:
         for h in range(2):
             if own is not None and own // HALF == h:
-                store(h, [(S.mine, 1), (arr[h], HALF - 1)])
+                store(h, [(S.mine, 1), (arr[h], ENG[h] * (HALF - 1))])
             else:
-                store(h, [(arr[h], HALF)])
+                store(h, [(arr[h], ENG[h] * HALF)])
         if own is not None:
             g.wait_ge(S.sent, 8)
         g.wait_ge(S.stA, 16)
@@ -106,8 +108,8 @@ def rank_program(g, core, T, topo):
         g.scalar.wait_ge(S.res2, 1)
         g.scalar.dma_start(T.y2[:], T.rs[:]).then_inc(S.st2, 16)
         hx = m // 2
-        got = S.arrA if hx == 0 else S.mine
-        g.wait_ge(got, 4)
+        got, ngot = (S.arrA, 4 * ENG[0]) if hx == 0 else (S.mine, 4)
+        g.wait_ge(got, ngot)
         g.remote_dma_fused(
             [RemoteDMATransfer(dst_ids=[did(s) for s in sibs], dma_engine_mask=0xF << (4 * j), remote_sem=fw[hx],
                                srcs=[T.buf[4 * m + j]], dsts=[T.buf[4 * m + j] for s in sibs])
@@ -115,7 +117,7 @@ def rank_program(g, core, T, topo):
             local_sem=S.sent)
         for h in range(2):
             if h == hx:
-                store(h, [(got, 4), (fw[h], 16)])
+                store(h, [(got, ngot), (fw[h], 16)])
             else:
                 store(h, [(fw[h], 32)])
         g.wait_ge(S.sent, 3 + 1 + 16)

from concourse.bass import DstId, RemoteDMATransfer

NP = 16
HALF = NP // 2
ENG = (4, 4)

SCRATCH = {
    "buf": ("dram", [NP, 128, 32], "float32"),
    "r": ("dram", [4, 128, 4], "float32"),
    "rs": ("dram", [128, 4], "float32"),
}
SEMAPHORES = ["ldA", "ldB", "mine", "arrA", "arrB", "fwA", "fwB", "sent", "stA", "stB", "ld2", "got2", "res2", "st2"]


def holder(p):
    if p == 0:
        return 128 + 6
    return 8 * p + (6 if p % 2 == 0 else 2)


def rank_program(g, core, T, topo):
    S = T.sem
    cores = list(T.cores)
    root = cores[T.tables["G1"][T.tables["ROOT1"]]]
    far = [cores[r] for r in T.tables["G2"]]
    near = [c for c in cores if c not in far and c != root]
    arr = (S.arrA, S.arrB)
    fw = (S.fwA, S.fwB)
    st = (S.stA, S.stB)
    queues = (g.sync, g.scalar)

    def did(dst):
        rid, pid = topo.addr(dst, core)
        return DstId(rid=rid, pnc=pid)

    def store(h, waits):
        q = queues[h]
        for sem, n in waits:
            q.wait_ge(sem, n)
        q.dma_start(T.y1[64 * h:64 * h + 64, :], T.buf[HALF * h:HALF * h + HALF]).then_inc(st[h], 16)

    if core == root:
        g.sync.dma_start(T.buf[0:HALF], T.x1[0:64, :]).then_inc(S.ldA, 16)
        g.scalar.dma_start(T.buf[HALF:NP], T.x1[64:128, :]).then_inc(S.ldB, 16)
        for h, ld in enumerate((S.ldA, S.ldB)):
            g.wait_ge(ld, 16)
            trs = []
            for p in range(HALF * h, HALF * h + HALF):
                to = [holder(p)] + ([far[p // 4]] if h == 1 else [])
                trs.append(RemoteDMATransfer(dst_ids=[did(d) for d in to], dma_engine_mask=1 << (p % 8), remote_sem=S.mine,
                                             srcs=[T.buf[p]], dsts=[T.buf[p] for d in to]))
            g.remote_dma_fused(trs, local_sem=S.sent)
        g.sync.wait_ge(S.sent, NP)
        g.sync.dma_start(T.y1[:], T.x1[:]).then_inc(S.stA, 16)
        g.wait_ge(S.sent, NP)
        g.wait_ge(S.stA, 16)
        return

    own = None
    for p in range(NP):
        if holder(p) == core:
            own = p
    if own is not None:
        others = [c for c in near if c != core]
        k = own % len(others)
        dests = others[k:] + others[:k]
        if own < HALF:
            dests = [far[own // 4]] + dests
        ne = ENG[own // HALF]
        nt = 8 // ne
        g.wait_ge(S.mine, 1)
        g.remote_dma_fused(
            [RemoteDMATransfer(dst_ids=[did(d) for d in dests[t::nt]], dma_engine_mask=((1 << ne) - 1) << (ne * t),
                               remote_sem=arr[own // HALF], srcs=[T.buf[own]], dsts=[T.buf[own] for d in dests[t::nt]])
             for t in range(nt)],
            local_sem=S.sent)
        if core not in near:
            g.wait_ge(S.sent, 8)
            return

    if core in near:
        for h in range(2):
            if own is not None and own // HALF == h:
                store(h, [(S.mine, 1), (arr[h], ENG[h] * (HALF - 1))])
            else:
                store(h, [(arr[h], ENG[h] * HALF)])
        if own is not None:
            g.wait_ge(S.sent, 8)
        g.wait_ge(S.stA, 16)
        g.wait_ge(S.stB, 16)
        return

    if core in far:
        m = far.index(core)
        sibs = [c for c in far if c != core]
        g.sync.dma_start(T.r[m], T.x2[:]).then_inc(S.ld2, 16)
        g.wait_ge(S.ld2, 16)
        g.remote_dma_fused(
            [RemoteDMATransfer(dst_ids=[did(s)], dma_engine_mask=1 << j, remote_sem=S.got2,
                               srcs=[T.r[m]], dsts=[T.r[m]])
             for j, s in enumerate(sibs)],
            local_sem=S.sent)
        g.wait_ge(S.got2, 3)
        g.remote_dma_fused(
            [RemoteDMATransfer(dst_ids=[did(far[(m + 1) % 4])], dma_engine_mask=1, remote_sem=S.res2,
                               srcs=[T.r[j] for j in range(4)], dsts=[T.rs[:]], alu_op=1)],
            local_sem=S.sent)
        g.scalar.wait_ge(S.res2, 1)
        g.scalar.dma_start(T.y2[:], T.rs[:]).then_inc(S.st2, 16)
        hx = m // 2
        got, ngot = (S.arrA, 4 * ENG[0]) if hx == 0 else (S.mine, 4)
        g.wait_ge(got, ngot)
        g.remote_dma_fused(
            [RemoteDMATransfer(dst_ids=[did(s) for s in sibs], dma_engine_mask=0xF << (4 * j), remote_sem=fw[hx],
                               srcs=[T.buf[4 * m + j]], dsts=[T.buf[4 * m + j] for s in sibs])
             for j in range(4)],
            local_sem=S.sent)
        for h in range(2):
            if h == hx:
                store(h, [(got, ngot), (fw[h], 16)])
            else:
                store(h, [(fw[h], 32)])
        g.wait_ge(S.sent, 3 + 1 + 16)
        g.wait_ge(S.st2, 16)
        g.wait_ge(S.stA, 16)
        g.wait_ge(S.stB, 16)
        return
